import numpy as np
import ml_dtypes


def mxq(x, axis, fmt="e4m3"):
    dtype, down = {"e4m3": (ml_dtypes.float8_e4m3fn, 7), "e5m2": (ml_dtypes.float8_e5m2, 14)}[fmt]
    v = np.moveaxis(np.asarray(x, np.float32).astype(ml_dtypes.bfloat16).astype(np.float64), axis, -1)
    blocks = v.reshape(v.shape[:-1] + (-1, 32))
    amax = np.abs(blocks).max(-1, keepdims=True)
    byte = np.maximum(np.where(amax > 0, np.frexp(amax)[1] - 1 + 127, 0) - down, 1)
    scale = np.exp2(byte - 127.0)
    codes = (blocks / scale).astype(np.float32).astype(dtype).astype(np.float64)
    return np.moveaxis((codes * scale).reshape(v.shape), -1, axis)


WIDE = False


def mx_kscale(k):
    if not WIDE:
        return np.ones(k)
    levels = np.array([10, -10, 5, -5, 0])
    if k % 512:
        return np.exp2(np.random.permutation(np.resize(levels, k // 32))).repeat(32)
    a = np.empty((k // 512, 16))
    for p in range(k // 512):
        a[p, :8] = np.random.permutation(np.resize(levels, 8))
        for g in range(8):
            far = levels[np.abs(levels - a[p, g]) >= 10]
            a[p, g + 8] = far[np.random.randint(len(far))]
    return np.exp2(a.ravel()).repeat(32)


def f64(x):
    return np.asarray(x).astype(np.float64)


def striped(idx):
    return np.tile(idx.reshape(-1, 16).T, (8, 1)).astype(np.uint16)


def unstriped(offs):
    return offs[:16].T.reshape(-1).astype(np.int64)


def striped8(idx):
    return np.concatenate([x.reshape(-1, 16).T for x in idx]).astype(np.uint16)


def runs(offs, k):
    lists = np.stack([offs[16 * r : 16 * r + 16].T.reshape(-1) for r in range(8)]).astype(np.int64)
    return lists[np.arange(k) % 512 // 64]


def pack_weight(w):
    k, n = w.shape
    w = f64(np.asarray(w, np.float32).astype(ml_dtypes.bfloat16)).reshape(k // 32, 32, n)
    amax = np.abs(w).max(1)
    byte = np.clip(np.where(amax > 0, np.frexp(amax)[1] - 1 + 127 - 7, 1), 1, 254)
    scaled = (w * np.exp2(127.0 - byte)[:, None, :]).reshape(k, n).astype(np.float32)
    words = np.ascontiguousarray(scaled.reshape(k // 512, 128, 4, n).transpose(0, 1, 3, 2)).astype(ml_dtypes.float8_e4m3fn).view(np.uint8)
    return words, np.ascontiguousarray(byte.astype(np.uint8).reshape(k // 512, 16, n))


def unpack_weight(words, scales):
    g, p, n, _ = words.shape
    vals = np.ascontiguousarray(words).view(ml_dtypes.float8_e4m3fn).astype(np.float64) * np.repeat(np.exp2(scales.astype(np.float64) - 127.0), 8, axis=1)[..., None]
    return vals.transpose(0, 1, 3, 2).reshape(g * 512, n)


def sigmoid(v):
    return 1.0 / (1.0 + np.exp(-np.maximum(v, -700.0)))


K, T, S, H = 512, 2048, 512, 512


def setup_inputs():
    n = np.random.standard_normal
    s = mx_kscale(K)[:, None]
    u = mx_kscale(S)
    packed_xT = pack_weight(n((K, T)) * s)
    return {
        "x_words": packed_xT[0],
        "x_scales": packed_xT[1],
        "w1": (n((K, H)) / np.sqrt(K) / s).astype(np.float32),
        "tau": np.random.uniform(0.3, 0.9, (H, 1)).astype(np.float32),
        "sl": np.random.uniform(1.0, 2.0, (H, 1)).astype(np.float32),
        "th": (0.5 * n((H, 1))).astype(np.float32),
        "ga": (np.random.uniform(0.5, 1.5, (H, 1)) * u[:, None]).astype(np.float32),
        "gb": (np.random.uniform(0.5, 1.5, (H, 1)) / u[:, None]).astype(np.float32),
        "sl2": np.random.uniform(1.5, 3.0, (S, 1)).astype(np.float32),
        "th2": (0.5 * n((S, 1))).astype(np.float32),
        "offs": striped(np.random.permutation(T)[:S]),
        "n1": striped(np.random.permutation(S)),
        "n2": striped(np.random.permutation(S)),
        "n3": striped8(np.stack([np.random.permutation(S) for _ in range(8)])),
        "n4": striped8(np.stack([np.random.permutation(S) for _ in range(8)])),
        "n5": striped8(np.stack([np.random.permutation(S) for _ in range(8)])),
        "n6": striped8(np.stack([np.random.permutation(S) for _ in range(8)])),
    }


def reference(x_words, x_scales, w1, tau, sl, th, ga, gb, sl2, th2, offs, n1, n2, n3, n4, n5, n6):
    xq = unpack_weight(x_words, x_scales)[:, unstriped(offs)]
    y = mxq(f64(w1), 0, "e4m3").T @ xq
    sq = (y) ** 2
    ea = np.exp(-1.0 * (f64(tau) * sq[:, unstriped(n1)]))
    z = f64(ga) * (y * ea - (0.5 * y[:, unstriped(n2)]))
    pa = y[np.arange(H)[:, None], runs(n3, H)]
    sg = sigmoid(f64(sl) * (y[np.arange(H)[:, None], runs(n4, H)] - f64(th)))
    z2 = f64(gb) * (pa + sg * (y - pa))
    s = 0.0625 * ((mxq(z, 0, "e4m3").T @ mxq(z2, 0, "e4m3")))
    sg2 = sigmoid(f64(sl2) * (s[np.arange(S)[:, None], runs(n5, S)] - f64(th2)))
    return 1.5 * (s * (sg2 - (sg2[np.arange(S)[:, None], runs(n6, S)])))

@@ -1,0 +1,213 @@
+from contextlib import ExitStack
+
+import concourse.mybir as mybir
+
+K, T, S, H = 512, 2048, 512, 512
+FLOPS = 2 * K * H * S + 2 * H * S * S
+
+F32 = mybir.dt.float32
+BF16 = mybir.dt.bfloat16
+I32 = mybir.dt.int32
+U32 = mybir.dt.uint32
+U16 = mybir.dt.uint16
+U8 = mybir.dt.uint8
+FP8X4 = mybir.dt.float8_e4m3fn_x4
+ALU = mybir.AluOpType
+ACT = mybir.ActivationFunctionType
+
+P = 128
+PACK = 4
+WIDE = 2 * S
+
+
+def tile_picked_selfegaebledb_none_p_kernel(tc, x_words, x_scales, w1, tau, sl, th, ga, gb, sl2, th2, offs, n1, n2, n3, n4, n5, n6, out):
+    nc = tc.nc
+    with ExitStack() as ctx:
+        keep = ctx.enter_context(tc.tile_pool(name="keep", bufs=1))
+        psum = ctx.enter_context(tc.psum_pool(name="psum", bufs=1))
+
+        def sbuf(name, shape, dtype):
+            return keep.tile(shape, dtype, name=name, align_bytes=64)
+
+        def four(name, shape, dtype):
+            return [sbuf("%s%d" % (name, t), shape, dtype) for t in range(PACK)]
+
+        def load_list(name, src):
+            tile = sbuf(name, [P, S // 16], U16)
+            nc.sync.dma_start(tile[:], src)
+            return tile
+
+        def load_rows(name, src):
+            tile = sbuf(name, [P, PACK], F32)
+            nc.sync.dma_start(out=tile[:], in_=src.rearrange("(p t) o -> p (t o)", t=PACK))
+            return tile
+
+        x_bytes = sbuf("x_bytes", [P, T], U8)
+        nc.vector.memset(x_bytes[:].bitcast(I32), 0)
+        offs_sb = load_list("offs_sb", offs)
+        w_raw = sbuf("w_raw", [P, PACK, H], F32)
+        nc.sync.dma_start(out=w_raw[:], in_=w1.rearrange("(p j) c -> p j c", j=PACK))
+        sl_sb = load_rows("sl_sb", sl)
+        th_sb = load_rows("th_sb", th)
+        x_packed = sbuf("x_packed", [P, T], U32)
+        nc.sync.dma_start(out=x_packed[:].bitcast(I32), in_=x_words[0].rearrange("p n r -> p (n r)").bitcast(I32))
+        for quad in range(4):
+            nc.scalar.dma_start(
+                out=x_bytes[32 * quad : 32 * quad + 4, :].bitcast(I32),
+                in_=x_scales[0, 4 * quad : 4 * quad + 4, :].bitcast(I32),
+            )
+        n4_sb = load_list("n4_sb", n4)
+        gb_sb = load_rows("gb_sb", gb)
+        n3_sb = load_list("n3_sb", n3)
+        tau_sb = load_rows("tau_sb", tau)
+        n1_sb = load_list("n1_sb", n1)
+        ga_sb = load_rows("ga_sb", ga)
+        n2_sb = load_list("n2_sb", n2)
+        sl2_sb = load_rows("sl2_sb", sl2)
+        th2_sb = load_rows("th2_sb", th2)
+        n5_sb = load_list("n5_sb", n5)
+        n6_sb = load_list("n6_sb", n6)
+
+        def times(name, src, factor):
+            tile = sbuf(name, [P, PACK], F32)
+            nc.gpsimd.tensor_scalar(tile[:], src[:], factor, 0.0, ALU.mult, ALU.add)
+            return tile
+
+        def minus_product(name, a, b):
+            neg = sbuf(name + "_neg", [P, PACK], F32)
+            nc.scalar.mul(neg[:], a[:], -1.0)
+            tile = sbuf(name, [P, PACK], F32)
+            nc.gpsimd.tensor_tensor(tile[:], neg[:], b[:], ALU.mult)
+            return tile
+
+        bias_sg = minus_product("bias_sg", sl_sb, th_sb)
+        neg_tau = times("neg_tau", tau_sb, -1.0)
+        half_ga = times("half_ga", ga_sb, -0.5)
+        neg_sl2 = times("neg_sl2", sl2_sb, -1.0)
+        bias_sg2 = sbuf("bias_sg2", [P, PACK], F32)
+        nc.gpsimd.tensor_tensor(bias_sg2[:], neg_sl2[:], th2_sb[:], ALU.mult)
+
+        y_win = four("y_win", [P, WIDE], F32)
+        sq_win = four("sq_win", [P, WIDE], F32)
+        s_win = four("s_win", [P, WIDE], F32)
+        sg2_win = four("sg2_win", [P, WIDE], F32)
+        for t in range(PACK):
+            nc.vector.memset(y_win[t][:, S:], 0.0)
+        sg = [sq_win[PACK - 1 - t][:, S:] for t in range(PACK)]
+        y_n2 = [s_win[t][:, S:] for t in range(PACK)]
+        ea = [sg2_win[t][:, S:] for t in range(PACK)]
+
+        xq_bytes = sbuf("xq_bytes", [P, S], U8)
+        nc.vector.tensor_copy(xq_bytes[:], x_bytes[:].indirect(offs_sb[:]))
+        w_bf = sbuf("w_bf", [P, H * PACK], BF16)
+        nc.vector.tensor_copy(
+            out=w_bf[:].rearrange("p (t m j) -> p m j t", t=PACK, j=PACK),
+            in_=w_raw[:].rearrange("p j (m t) -> p m j t", t=PACK),
+        )
+        w_codes = sbuf("w_codes", [P, H], U32)
+        w_scales = sbuf("w_scales", [P, H], U8)
+        nc.vector.quantize_mx(out=w_codes[:].bitcast(FP8X4), scales=w_scales[:], in_=w_bf[:])
+        xq_words = sbuf("xq_words", [P, S], U32)
+        nc.vector.tensor_copy(xq_words[:], x_packed[:].indirect(offs_sb[:]))
+
+        y_ps = [psum.tile([P, S], F32, name="y_ps%d" % t) for t in range(PACK)]
+        for t in range(PACK):
+            cols = slice(P * t, P * (t + 1))
+            nc.tensor.matmul_mx(
+                out=y_ps[t][:],
+                lhsT=w_codes[:, cols].bitcast(FP8X4),
+                lhsT_scale=w_scales[:, cols],
+                rhs=xq_words[:].bitcast(FP8X4),
+                rhs_scale=xq_bytes[:],
+                start=True,
+                stop=True,
+            )
+        for t in range(PACK):
+            nc.vector.tensor_copy(y_win[t][:, :S], y_ps[t][:])
+
+        kept = sbuf("kept", [P, PACK, S], F32)
+        fetched = sbuf("fetched", [P, PACK, S], F32)
+        rest = four("rest", [P, S], F32)
+        for t in range(PACK):
+            col = slice(t, t + 1)
+            nc.scalar.activation(sg[t], y_win[t][:].indirect(n4_sb[:]), ACT.Sigmoid, bias=bias_sg[:, col], scale=sl_sb[:, col])
+        for t in range(PACK - 1):
+            nc.scalar.activation(sq_win[t][:, :S], y_win[t][:, :S], ACT.Square)
+        for t in range(PACK):
+            col = slice(t, t + 1)
+            nc.vector.tensor_scalar(rest[t][:], sg[t], 1.0, gb_sb[:, col], ALU.subtract, ALU.mult)
+            nc.vector.scalar_tensor_tensor(kept[:, t, :], y_ps[t][:], gb_sb[:, col], sg[t], ALU.mult, ALU.mult)
+            nc.vector.tensor_tensor(fetched[:, t, :], y_win[t][:].indirect(n3_sb[:]), rest[t][:], ALU.mult)
+        nc.vector.tensor_tensor(sq_win[PACK - 1][:, :S], y_ps[PACK - 1][:], y_win[PACK - 1][:, :S], ALU.mult)
+        z2_bf = sbuf("z2_bf", [P, S * PACK], BF16)
+        nc.vector.tensor_tensor(
+            z2_bf[:].rearrange("p (c i t) -> p c t i", i=4, t=PACK),
+            kept[:].rearrange("p t (c i) -> p c t i", i=4),
+            fetched[:].rearrange("p t (c i) -> p c t i", i=4),
+            ALU.subtract,
+        )
+        z2_codes = sbuf("z2_codes", [P, S], U32)
+        z2_scales = sbuf("z2_scales", [P, S], U8)
+
+        for t in range(PACK):
+            nc.scalar.activation(ea[t], sq_win[t][:].indirect(n1_sb[:]), ACT.Exp, scale=neg_tau[:, t : t + 1])
+        for t in range(PACK):
+            nc.scalar.activation(y_n2[t], y_win[t][:].indirect(n2_sb[:]), ACT.Copy)
+        damped = four("damped", [P, S], F32)
+        z_rows = sbuf("z_rows", [P, PACK, S], BF16)
+        for t in range(PACK):
+            nc.vector.scalar_tensor_tensor(damped[t][:], y_ps[t][:], ga_sb[:, t : t + 1], ea[t], ALU.mult, ALU.mult)
+            if t == 0:
+                nc.vector.quantize_mx(out=z2_codes[:].bitcast(FP8X4), scales=z2_scales[:], in_=z2_bf[:])
+        for t in range(PACK):
+            nc.vector.scalar_tensor_tensor(
+                z_rows[:, t, :].rearrange("p (u m) -> p m u", u=PACK),
+                y_n2[t].rearrange("p (m u) -> p m u", u=PACK),
+                half_ga[:, t : t + 1],
+                damped[t][:].rearrange("p (m u) -> p m u", u=PACK),
+                ALU.mult,
+                ALU.add,
+            )
+
+        z_bf = four("z_bf", [P, P * PACK], BF16)
+        z_codes = four("z_codes", [P, P], U32)
+        z_scales = four("z_scales", [P, P], U8)
+        s_ps = [psum.tile([P, S], F32, name="s_ps%d" % u) for u in range(PACK)]
+        for u in range(PACK):
+            nc.vector.tensor_copy(
+                out=z_bf[u][:].rearrange("p (c i t) -> p c t i", i=4, t=PACK),
+                in_=z_rows[:, :, P * u : P * (u + 1)].rearrange("p t (c i) -> p c t i", i=4),
+            )
+            nc.vector.quantize_mx(out=z_codes[u][:].bitcast(FP8X4), scales=z_scales[u][:], in_=z_bf[u][:])
+            nc.tensor.matmul_mx(
+                out=s_ps[u][:],
+                lhsT=z_codes[u][:].bitcast(FP8X4),
+                lhsT_scale=z_scales[u][:],
+                rhs=z2_codes[:].bitcast(FP8X4),
+                rhs_scale=z2_scales[:],
+                start=True,
+                stop=True,
+            )
+            nc.vector.tensor_scalar(s_win[u][:, :S], s_ps[u][:], 0.0625, None, ALU.mult)
+
+        sg2_n6 = four("sg2_n6", [P, S], F32)
+        diff = four("diff", [P, S], F32)
+        res = four("res", [P, S], F32)
+        out_rows = out.rearrange("(p u) c -> u p c", u=PACK)
+
+        def gate(u):
+            col = slice(u, u + 1)
+            nc.scalar.activation(sg2_win[u][:, :S], s_win[u][:].indirect(n5_sb[:]), ACT.Sigmoid, bias=bias_sg2[:, col], scale=sl2_sb[:, col])
+
+        def finish(u, lo, hi):
+            nc.scalar.activation(sg2_n6[u][:, lo:hi], sg2_win[u][:].indirect(n6_sb[:, lo // 16 : hi // 16]), ACT.Copy)
+            nc.vector.tensor_tensor(diff[u][:, lo:hi], sg2_win[u][:, lo:hi], sg2_n6[u][:, lo:hi], ALU.subtract)
+            nc.vector.scalar_tensor_tensor(res[u][:, lo:hi], diff[u][:, lo:hi], 1.5, s_win[u][:, lo:hi], ALU.mult, ALU.mult)
+            nc.sync.dma_start(out=out_rows[u][:, lo:hi], in_=res[u][:, lo:hi])
+
+        gate(0)
+        for u in range(PACK - 1):
+            gate(u + 1)
+            finish(u, 0, S)
+        finish(PACK - 1, 0, S // 2)
+        finish(PACK - 1, S // 2, S)

@@ -81,6 +81,8 @@ def tile_picked_selfegaebledb_none_p_kernel(tc, x_words, x_scales, w1, tau, sl, 
             return tile
 
         bias_sg = minus_product("bias_sg", sl_sb, th_sb)
+        warm0 = sbuf("warm0", [P, 1], F32)
+        nc.scalar.activation(warm0[:], bias_sg[:, 0:1], ACT.Sigmoid)
         neg_tau = times("neg_tau", tau_sb, -1.0)
         half_ga = times("half_ga", ga_sb, -0.5)
         neg_sl2 = times("neg_sl2", sl2_sb, -1.0)
@@ -153,6 +155,8 @@ def tile_picked_selfegaebledb_none_p_kernel(tc, x_words, x_scales, w1, tau, sl, 
             nc.scalar.activation(ea[t], sq_win[t][:].indirect(n1_sb[:]), ACT.Exp, scale=neg_tau[:, t : t + 1])
         for t in range(PACK):
             nc.scalar.activation(y_n2[t], y_win[t][:].indirect(n2_sb[:]), ACT.Copy)
+        warm1 = sbuf("warm1", [P, 1], F32)
+        nc.scalar.activation(warm1[:], y_n2[PACK - 1][:, 0:1], ACT.Sigmoid)
         damped = four("damped", [P, S], F32)
         z_rows = sbuf("z_rows", [P, PACK, S], BF16)
         for t in range(PACK):

@@ -18,6 +18,7 @@ ACT = mybir.ActivationFunctionType
 P = 128
 PACK = 4
 WIDE = 2 * S
+W_SPLIT = 56
 
 
 def tile_picked_selfegaebledb_none_p_kernel(tc, x_words, x_scales, w1, tau, sl, th, ga, gb, sl2, th2, offs, n1, n2, n3, n4, n5, n6, out):
@@ -74,20 +75,16 @@ def tile_picked_selfegaebledb_none_p_kernel(tc, x_words, x_scales, w1, tau, sl, 
             return tile
 
         def minus_product(name, a, b):
-            neg = sbuf(name + "_neg", [P, PACK], F32)
-            nc.scalar.mul(neg[:], a[:], -1.0)
+            neg = times(name + "_neg", a, -1.0)
             tile = sbuf(name, [P, PACK], F32)
             nc.gpsimd.tensor_tensor(tile[:], neg[:], b[:], ALU.mult)
             return tile
 
         bias_sg = minus_product("bias_sg", sl_sb, th_sb)
-        warm0 = sbuf("warm0", [P, 1], F32)
-        nc.scalar.activation(warm0[:], bias_sg[:, 0:1], ACT.Sigmoid)
+        neg_gb = times("neg_gb", gb_sb, -1.0)
         neg_tau = times("neg_tau", tau_sb, -1.0)
         half_ga = times("half_ga", ga_sb, -0.5)
-        neg_sl2 = times("neg_sl2", sl2_sb, -1.0)
-        bias_sg2 = sbuf("bias_sg2", [P, PACK], F32)
-        nc.gpsimd.tensor_tensor(bias_sg2[:], neg_sl2[:], th2_sb[:], ALU.mult)
+        bias_sg2 = minus_product("bias_sg2", sl2_sb, th2_sb)
 
         y_win = four("y_win", [P, WIDE], F32)
         sq_win = four("sq_win", [P, WIDE], F32)
@@ -95,6 +92,8 @@ def tile_picked_selfegaebledb_none_p_kernel(tc, x_words, x_scales, w1, tau, sl, 
         sg2_win = four("sg2_win", [P, WIDE], F32)
         for t in range(PACK):
             nc.vector.memset(y_win[t][:, S:], 0.0)
+        warm0 = sbuf("warm0", [P, 1], F32)
+        nc.scalar.activation(warm0[:], y_win[0][:, S : S + 1], ACT.Sigmoid)
         sg = [sq_win[PACK - 1 - t][:, S:] for t in range(PACK)]
         y_n2 = [s_win[t][:, S:] for t in range(PACK)]
         ea = [sg2_win[t][:, S:] for t in range(PACK)]
@@ -102,10 +101,10 @@ def tile_picked_selfegaebledb_none_p_kernel(tc, x_words, x_scales, w1, tau, sl, 
         xq_bytes = sbuf("xq_bytes", [P, S], U8)
         nc.vector.tensor_copy(xq_bytes[:], x_bytes[:].indirect(offs_sb[:]))
         w_bf = sbuf("w_bf", [P, H * PACK], BF16)
-        nc.vector.tensor_copy(
-            out=w_bf[:].rearrange("p (t m j) -> p m j t", t=PACK, j=PACK),
-            in_=w_raw[:].rearrange("p j (m t) -> p m j t", t=PACK),
-        )
+        w_dealt = w_bf[:].rearrange("p (t m j) -> p m j t", t=PACK, j=PACK)
+        w_plain = w_raw[:].rearrange("p j (m t) -> p m j t", t=PACK)
+        nc.scalar.copy(out=w_dealt[:, :W_SPLIT], in_=w_plain[:, :W_SPLIT])
+        nc.vector.tensor_copy(out=w_dealt[:, W_SPLIT:], in_=w_plain[:, W_SPLIT:])
         w_codes = sbuf("w_codes", [P, H], U32)
         w_scales = sbuf("w_scales", [P, H], U8)
         nc.vector.quantize_mx(out=w_codes[:].bitcast(FP8X4), scales=w_scales[:], in_=w_bf[:])
@@ -124,7 +123,8 @@ def tile_picked_selfegaebledb_none_p_kernel(tc, x_words, x_scales, w1, tau, sl, 
                 start=True,
                 stop=True,
             )
-        for t in range(PACK):
+        nc.scalar.copy(y_win[0][:, :S], y_ps[0][:])
+        for t in range(1, PACK):
             nc.vector.tensor_copy(y_win[t][:, :S], y_ps[t][:])
 
         kept = sbuf("kept", [P, PACK, S], F32)
@@ -133,14 +133,13 @@ def tile_picked_selfegaebledb_none_p_kernel(tc, x_words, x_scales, w1, tau, sl, 
         for t in range(PACK):
             col = slice(t, t + 1)
             nc.scalar.activation(sg[t], y_win[t][:].indirect(n4_sb[:]), ACT.Sigmoid, bias=bias_sg[:, col], scale=sl_sb[:, col])
-        for t in range(PACK - 1):
+        for t in range(PACK):
             nc.scalar.activation(sq_win[t][:, :S], y_win[t][:, :S], ACT.Square)
         for t in range(PACK):
             col = slice(t, t + 1)
-            nc.vector.tensor_scalar(rest[t][:], sg[t], 1.0, gb_sb[:, col], ALU.subtract, ALU.mult)
+            nc.gpsimd.tensor_scalar(rest[t][:], sg[t], gb_sb[:, col], neg_gb[:, col], ALU.mult, ALU.add)
             nc.vector.scalar_tensor_tensor(kept[:, t, :], y_ps[t][:], gb_sb[:, col], sg[t], ALU.mult, ALU.mult)
             nc.vector.tensor_tensor(fetched[:, t, :], y_win[t][:].indirect(n3_sb[:]), rest[t][:], ALU.mult)
-        nc.vector.tensor_tensor(sq_win[PACK - 1][:, :S], y_ps[PACK - 1][:], y_win[PACK - 1][:, :S], ALU.mult)
         z2_bf = sbuf("z2_bf", [P, S * PACK], BF16)
         nc.vector.tensor_tensor(
             z2_bf[:].rearrange("p (c i t) -> p c t i", i=4, t=PACK),
@@ -153,22 +152,23 @@ def tile_picked_selfegaebledb_none_p_kernel(tc, x_words, x_scales, w1, tau, sl, 
 
         for t in range(PACK):
             nc.scalar.activation(ea[t], sq_win[t][:].indirect(n1_sb[:]), ACT.Exp, scale=neg_tau[:, t : t + 1])
-        for t in range(PACK):
-            nc.scalar.activation(y_n2[t], y_win[t][:].indirect(n2_sb[:]), ACT.Copy)
+        pieces = [(t, 0, S) for t in range(PACK - 1)] + [(PACK - 1, 0, S // 2), (PACK - 1, S // 2, S)]
+        for t, lo, hi in pieces:
+            nc.scalar.activation(y_n2[t][:, lo:hi], y_win[t][:].indirect(n2_sb[:, lo // 16 : hi // 16]), ACT.Copy)
         warm1 = sbuf("warm1", [P, 1], F32)
-        nc.scalar.activation(warm1[:], y_n2[PACK - 1][:, 0:1], ACT.Sigmoid)
+        nc.scalar.activation(warm1[:], y_n2[PACK - 1][:, S - 1 : S], ACT.Sigmoid)
         damped = four("damped", [P, S], F32)
         z_rows = sbuf("z_rows", [P, PACK, S], BF16)
         for t in range(PACK):
             nc.vector.scalar_tensor_tensor(damped[t][:], y_ps[t][:], ga_sb[:, t : t + 1], ea[t], ALU.mult, ALU.mult)
             if t == 0:
                 nc.vector.quantize_mx(out=z2_codes[:].bitcast(FP8X4), scales=z2_scales[:], in_=z2_bf[:])
-        for t in range(PACK):
+        for t, lo, hi in pieces:
             nc.vector.scalar_tensor_tensor(
-                z_rows[:, t, :].rearrange("p (u m) -> p m u", u=PACK),
-                y_n2[t].rearrange("p (m u) -> p m u", u=PACK),
+                z_rows[:, t, :].rearrange("p (u m) -> p m u", u=PACK)[:, lo // PACK : hi // PACK],
+                y_n2[t][:, lo:hi].rearrange("p (m u) -> p m u", u=PACK),
                 half_ga[:, t : t + 1],
-                damped[t][:].rearrange("p (m u) -> p m u", u=PACK),
+                damped[t][:, lo:hi].rearrange("p (m u) -> p m u", u=PACK),
                 ALU.mult,
                 ALU.add,
             )
@@ -177,22 +177,34 @@ def tile_picked_selfegaebledb_none_p_kernel(tc, x_words, x_scales, w1, tau, sl, 
         z_codes = four("z_codes", [P, P], U32)
         z_scales = four("z_scales", [P, P], U8)
         s_ps = [psum.tile([P, S], F32, name="s_ps%d" % u) for u in range(PACK)]
-        for u in range(PACK):
+        def pack_z(u, lo, hi):
             nc.vector.tensor_copy(
-                out=z_bf[u][:].rearrange("p (c i t) -> p c t i", i=4, t=PACK),
-                in_=z_rows[:, :, P * u : P * (u + 1)].rearrange("p t (c i) -> p c t i", i=4),
+                out=z_bf[u][:, PACK * lo : PACK * hi].rearrange("p (c i t) -> p c t i", i=4, t=PACK),
+                in_=z_rows[:, :, P * u + lo : P * u + hi].rearrange("p t (c i) -> p c t i", i=4),
             )
-            nc.vector.quantize_mx(out=z_codes[u][:].bitcast(FP8X4), scales=z_scales[u][:], in_=z_bf[u][:])
+            nc.vector.quantize_mx(
+                out=z_codes[u][:, lo:hi].bitcast(FP8X4), scales=z_scales[u][:, lo:hi], in_=z_bf[u][:, PACK * lo : PACK * hi]
+            )
+
+        def product(u, bank, lo, hi):
             nc.tensor.matmul_mx(
-                out=s_ps[u][:],
+                out=bank[:, lo:hi],
                 lhsT=z_codes[u][:].bitcast(FP8X4),
                 lhsT_scale=z_scales[u][:],
-                rhs=z2_codes[:].bitcast(FP8X4),
-                rhs_scale=z2_scales[:],
+                rhs=z2_codes[:, lo:hi].bitcast(FP8X4),
+                rhs_scale=z2_scales[:, lo:hi],
                 start=True,
                 stop=True,
             )
-            nc.vector.tensor_scalar(s_win[u][:, :S], s_ps[u][:], 0.0625, None, ALU.mult)
+            nc.vector.tensor_scalar(s_win[u][:, lo:hi], bank[:, lo:hi], 0.0625, None, ALU.mult)
+
+        pack_z(0, 0, P // 2)
+        pack_z(0, P // 2, P)
+        product(0, s_ps[0], 0, S // 2)
+        product(0, y_ps[0], S // 2, S)
+        for u in range(1, PACK):
+            pack_z(u, 0, P)
+            product(u, s_ps[u], 0, S)
 
         sg2_n6 = four("sg2_n6", [P, S], F32)
         diff = four("diff", [P, S], F32)
@@ -210,8 +222,12 @@ def tile_picked_selfegaebledb_none_p_kernel(tc, x_words, x_scales, w1, tau, sl, 
             nc.sync.dma_start(out=out_rows[u][:, lo:hi], in_=res[u][:, lo:hi])
 
         gate(0)
-        for u in range(PACK - 1):
-            gate(u + 1)
-            finish(u, 0, S)
-        finish(PACK - 1, 0, S // 2)
-        finish(PACK - 1, S // 2, S)
+        gate(1)
+        finish(0, 0, S)
+        gate(2)
+        finish(1, 0, S)
+        finish(2, 0, S // 2)
+        gate(3)
+        finish(2, S // 2, S)
+        finish(3, 0, S // 2)
+        finish(3, S // 2, S)

@@ -18,7 +18,6 @@ ACT = mybir.ActivationFunctionType
 P = 128
 PACK = 4
 WIDE = 2 * S
-W_SPLIT = 56
 
 
 def tile_picked_selfegaebledb_none_p_kernel(tc, x_words, x_scales, w1, tau, sl, th, ga, gb, sl2, th2, offs, n1, n2, n3, n4, n5, n6, out):
@@ -81,7 +80,6 @@ def tile_picked_selfegaebledb_none_p_kernel(tc, x_words, x_scales, w1, tau, sl, 
             return tile
 
         bias_sg = minus_product("bias_sg", sl_sb, th_sb)
-        neg_gb = times("neg_gb", gb_sb, -1.0)
         neg_tau = times("neg_tau", tau_sb, -1.0)
         half_ga = times("half_ga", ga_sb, -0.5)
         bias_sg2 = minus_product("bias_sg2", sl2_sb, th2_sb)
@@ -101,10 +99,9 @@ def tile_picked_selfegaebledb_none_p_kernel(tc, x_words, x_scales, w1, tau, sl, 
         xq_bytes = sbuf("xq_bytes", [P, S], U8)
         nc.vector.tensor_copy(xq_bytes[:], x_bytes[:].indirect(offs_sb[:]))
         w_bf = sbuf("w_bf", [P, H * PACK], BF16)
-        w_dealt = w_bf[:].rearrange("p (t m j) -> p m j t", t=PACK, j=PACK)
-        w_plain = w_raw[:].rearrange("p j (m t) -> p m j t", t=PACK)
-        nc.scalar.copy(out=w_dealt[:, :W_SPLIT], in_=w_plain[:, :W_SPLIT])
-        nc.vector.tensor_copy(out=w_dealt[:, W_SPLIT:], in_=w_plain[:, W_SPLIT:])
+        w_dealt = w_bf[:].rearrange("p (a e m j) -> p a m j e", a=2, e=2, j=PACK)
+        w_plain = w_raw[:].rearrange("p j (m a e) -> p a m j e", a=2, e=2)
+        nc.vector.tensor_copy(out=w_dealt, in_=w_plain)
         w_codes = sbuf("w_codes", [P, H], U32)
         w_scales = sbuf("w_scales", [P, H], U8)
         nc.vector.quantize_mx(out=w_codes[:].bitcast(FP8X4), scales=w_scales[:], in_=w_bf[:])
@@ -133,18 +130,19 @@ def tile_picked_selfegaebledb_none_p_kernel(tc, x_words, x_scales, w1, tau, sl, 
         for t in range(PACK):
             col = slice(t, t + 1)
             nc.scalar.activation(sg[t], y_win[t][:].indirect(n4_sb[:]), ACT.Sigmoid, bias=bias_sg[:, col], scale=sl_sb[:, col])
-        for t in range(PACK):
+        for t in range(PACK - 1):
             nc.scalar.activation(sq_win[t][:, :S], y_win[t][:, :S], ACT.Square)
         for t in range(PACK):
             col = slice(t, t + 1)
-            nc.gpsimd.tensor_scalar(rest[t][:], sg[t], gb_sb[:, col], neg_gb[:, col], ALU.mult, ALU.add)
+            nc.vector.tensor_scalar(rest[t][:], sg[t], 1.0, gb_sb[:, col], ALU.subtract, ALU.mult)
             nc.vector.scalar_tensor_tensor(kept[:, t, :], y_ps[t][:], gb_sb[:, col], sg[t], ALU.mult, ALU.mult)
             nc.vector.tensor_tensor(fetched[:, t, :], y_win[t][:].indirect(n3_sb[:]), rest[t][:], ALU.mult)
+        nc.vector.tensor_tensor(sq_win[PACK - 1][:, :S], y_ps[PACK - 1][:], y_win[PACK - 1][:, :S], ALU.mult)
         z2_bf = sbuf("z2_bf", [P, S * PACK], BF16)
         nc.vector.tensor_tensor(
-            z2_bf[:].rearrange("p (c i t) -> p c t i", i=4, t=PACK),
-            kept[:].rearrange("p t (c i) -> p c t i", i=4),
-            fetched[:].rearrange("p t (c i) -> p c t i", i=4),
+            z2_bf[:].rearrange("p (c i t) -> p c t i", i=2, t=PACK),
+            kept[:].rearrange("p t (c i) -> p c t i", i=2),
+            fetched[:].rearrange("p t (c i) -> p c t i", i=2),
             ALU.subtract,
         )
         z2_codes = sbuf("z2_codes", [P, S], U32)
@@ -158,20 +156,24 @@ def tile_picked_selfegaebledb_none_p_kernel(tc, x_words, x_scales, w1, tau, sl, 
         warm1 = sbuf("warm1", [P, 1], F32)
         nc.scalar.activation(warm1[:], y_n2[PACK - 1][:, S - 1 : S], ACT.Sigmoid)
         damped = four("damped", [P, S], F32)
-        z_rows = sbuf("z_rows", [P, PACK, S], BF16)
+        z_rows = [sbuf("z_rows%d" % a, [P, PACK, S // 2], BF16) for a in range(2)]
         for t in range(PACK):
             nc.vector.scalar_tensor_tensor(damped[t][:], y_ps[t][:], ga_sb[:, t : t + 1], ea[t], ALU.mult, ALU.mult)
             if t == 0:
                 nc.vector.quantize_mx(out=z2_codes[:].bitcast(FP8X4), scales=z2_scales[:], in_=z2_bf[:])
-        for t, lo, hi in pieces:
+
+        def sum_z(a, t, lo, hi):
             nc.vector.scalar_tensor_tensor(
-                z_rows[:, t, :].rearrange("p (u m) -> p m u", u=PACK)[:, lo // PACK : hi // PACK],
-                y_n2[t][:, lo:hi].rearrange("p (m u) -> p m u", u=PACK),
+                z_rows[a][:, t, :].rearrange("p (e m) -> p m e", e=2)[:, lo // PACK : hi // PACK],
+                y_n2[t][:, lo:hi].rearrange("p (m u) -> p m u", u=PACK)[:, :, 2 * a : 2 * a + 2],
                 half_ga[:, t : t + 1],
-                damped[t][:, lo:hi].rearrange("p (m u) -> p m u", u=PACK),
+                damped[t][:, lo:hi].rearrange("p (m u) -> p m u", u=PACK)[:, :, 2 * a : 2 * a + 2],
                 ALU.mult,
                 ALU.add,
             )
+
+        for t, lo, hi in pieces:
+            sum_z(0, t, lo, hi)
 
         z_bf = four("z_bf", [P, P * PACK], BF16)
         z_codes = four("z_codes", [P, P], U32)
@@ -180,7 +182,7 @@ def tile_picked_selfegaebledb_none_p_kernel(tc, x_words, x_scales, w1, tau, sl, 
         def pack_z(u, lo, hi):
             nc.vector.tensor_copy(
                 out=z_bf[u][:, PACK * lo : PACK * hi].rearrange("p (c i t) -> p c t i", i=4, t=PACK),
-                in_=z_rows[:, :, P * u + lo : P * u + hi].rearrange("p t (c i) -> p c t i", i=4),
+                in_=z_rows[u // 2][:, :, P * (u % 2) + lo : P * (u % 2) + hi].rearrange("p t (c i) -> p c t i", i=4),
             )
             nc.vector.quantize_mx(
                 out=z_codes[u][:, lo:hi].bitcast(FP8X4), scales=z_scales[u][:, lo:hi], in_=z_bf[u][:, PACK * lo : PACK * hi]
@@ -203,11 +205,14 @@ def tile_picked_selfegaebledb_none_p_kernel(tc, x_words, x_scales, w1, tau, sl, 
         product(0, s_ps[0], 0, S // 2)
         product(0, y_ps[0], S // 2, S)
         for u in range(1, PACK):
+            if u == 2:
+                for t in range(PACK):
+                    sum_z(1, t, 0, S)
             pack_z(u, 0, P)
             product(u, s_ps[u], 0, S)
 
         sg2_n6 = four("sg2_n6", [P, S], F32)
-        diff = four("diff", [P, S], F32)
+        diff = [sbuf("z_rows1", [P, S], F32)] + [sbuf("diff%d" % u, [P, S], F32) for u in range(1, PACK)]
         res = four("res", [P, S], F32)
         out_rows = out.rearrange("(p u) c -> u p c", u=PACK)
 

@@ -17,7 +17,10 @@ ACT = mybir.ActivationFunctionType
 
 P = 128
 PACK = 4
+GROUP = 16
 WIDE = 2 * S
+W_SPLIT = 56
+HALVES = ((0, S // 2), (S // 2, S))
 
 
 def tile_picked_selfegaebledb_none_p_kernel(tc, x_words, x_scales, w1, tau, sl, th, ga, gb, sl2, th2, offs, n1, n2, n3, n4, n5, n6, out):
@@ -33,7 +36,7 @@ def tile_picked_selfegaebledb_none_p_kernel(tc, x_words, x_scales, w1, tau, sl, 
             return [sbuf("%s%d" % (name, t), shape, dtype) for t in range(PACK)]
 
         def load_list(name, src):
-            tile = sbuf(name, [P, S // 16], U16)
+            tile = sbuf(name, [P, S // GROUP], U16)
             nc.sync.dma_start(tile[:], src)
             return tile
 
@@ -90,8 +93,8 @@ def tile_picked_selfegaebledb_none_p_kernel(tc, x_words, x_scales, w1, tau, sl, 
         sg2_win = four("sg2_win", [P, WIDE], F32)
         for t in range(PACK):
             nc.vector.memset(y_win[t][:, S:], 0.0)
-        warm0 = sbuf("warm0", [P, 1], F32)
-        nc.scalar.activation(warm0[:], y_win[0][:, S : S + 1], ACT.Sigmoid)
+        preload_first = sbuf("preload_first", [P, 1], F32)
+        nc.scalar.activation(preload_first[:], y_win[0][:, S : S + 1], ACT.Sigmoid)
         sg = [sq_win[PACK - 1 - t][:, S:] for t in range(PACK)]
         y_n2 = [s_win[t][:, S:] for t in range(PACK)]
         ea = [sg2_win[t][:, S:] for t in range(PACK)]
@@ -101,26 +104,39 @@ def tile_picked_selfegaebledb_none_p_kernel(tc, x_words, x_scales, w1, tau, sl, 
         w_bf = sbuf("w_bf", [P, H * PACK], BF16)
         w_dealt = w_bf[:].rearrange("p (a e m j) -> p a m j e", a=2, e=2, j=PACK)
         w_plain = w_raw[:].rearrange("p j (m a e) -> p a m j e", a=2, e=2)
-        nc.vector.tensor_copy(out=w_dealt, in_=w_plain)
+        nc.scalar.copy(
+            out=w_bf[:].rearrange("p (t m j) -> p m j t", t=PACK, j=PACK)[:, :W_SPLIT],
+            in_=w_raw[:].rearrange("p j (m t) -> p m j t", t=PACK)[:, :W_SPLIT],
+        )
+        nc.vector.tensor_copy(out=w_dealt[:, :, W_SPLIT:], in_=w_plain[:, :, W_SPLIT:])
         w_codes = sbuf("w_codes", [P, H], U32)
         w_scales = sbuf("w_scales", [P, H], U8)
         nc.vector.quantize_mx(out=w_codes[:].bitcast(FP8X4), scales=w_scales[:], in_=w_bf[:])
         xq_words = sbuf("xq_words", [P, S], U32)
-        nc.vector.tensor_copy(xq_words[:], x_packed[:].indirect(offs_sb[:]))
+        for lo, hi in HALVES:
+            nc.vector.tensor_copy(xq_words[:, lo:hi], x_packed[:].indirect(offs_sb[:, lo // GROUP : hi // GROUP]))
 
         y_ps = [psum.tile([P, S], F32, name="y_ps%d" % t) for t in range(PACK)]
-        for t in range(PACK):
+        s_ps = [psum.tile([P, S], F32, name="s_ps%d" % u) for u in range(PACK)]
+
+        def project(t, bank, lo, hi):
             cols = slice(P * t, P * (t + 1))
             nc.tensor.matmul_mx(
-                out=y_ps[t][:],
+                out=bank[:, lo:hi],
                 lhsT=w_codes[:, cols].bitcast(FP8X4),
                 lhsT_scale=w_scales[:, cols],
-                rhs=xq_words[:].bitcast(FP8X4),
-                rhs_scale=xq_bytes[:],
+                rhs=xq_words[:, lo:hi].bitcast(FP8X4),
+                rhs_scale=xq_bytes[:, lo:hi],
                 start=True,
                 stop=True,
             )
-        nc.scalar.copy(y_win[0][:, :S], y_ps[0][:])
+
+        for bank, (lo, hi) in zip((s_ps[0], y_ps[0]), HALVES):
+            project(0, bank, lo, hi)
+            nc.scalar.copy(y_win[0][:, lo:hi], bank[:, lo:hi])
+        for t in range(1, PACK):
+            project(t, y_ps[t], 0, S)
+        y = [y_win[0][:, :S]] + [y_ps[t][:] for t in range(1, PACK)]
         for t in range(1, PACK):
             nc.vector.tensor_copy(y_win[t][:, :S], y_ps[t][:])
 
@@ -130,14 +146,14 @@ def tile_picked_selfegaebledb_none_p_kernel(tc, x_words, x_scales, w1, tau, sl, 
         for t in range(PACK):
             col = slice(t, t + 1)
             nc.scalar.activation(sg[t], y_win[t][:].indirect(n4_sb[:]), ACT.Sigmoid, bias=bias_sg[:, col], scale=sl_sb[:, col])
-        for t in range(PACK - 1):
-            nc.scalar.activation(sq_win[t][:, :S], y_win[t][:, :S], ACT.Square)
+        nc.gpsimd.tensor_tensor(sq_win[0][:, :S], y_win[0][:, :S], y_win[0][:, :S], ALU.mult)
+        for t in range(1, PACK):
+            nc.vector.tensor_tensor(sq_win[t][:, :S], y_ps[t][:], y_win[t][:, :S], ALU.mult)
         for t in range(PACK):
             col = slice(t, t + 1)
             nc.vector.tensor_scalar(rest[t][:], sg[t], 1.0, gb_sb[:, col], ALU.subtract, ALU.mult)
-            nc.vector.scalar_tensor_tensor(kept[:, t, :], y_ps[t][:], gb_sb[:, col], sg[t], ALU.mult, ALU.mult)
+            nc.vector.scalar_tensor_tensor(kept[:, t, :], y[t], gb_sb[:, col], sg[t], ALU.mult, ALU.mult)
             nc.vector.tensor_tensor(fetched[:, t, :], y_win[t][:].indirect(n3_sb[:]), rest[t][:], ALU.mult)
-        nc.vector.tensor_tensor(sq_win[PACK - 1][:, :S], y_ps[PACK - 1][:], y_win[PACK - 1][:, :S], ALU.mult)
         z2_bf = sbuf("z2_bf", [P, S * PACK], BF16)
         nc.vector.tensor_tensor(
             z2_bf[:].rearrange("p (c i t) -> p c t i", i=2, t=PACK),
@@ -152,13 +168,13 @@ def tile_picked_selfegaebledb_none_p_kernel(tc, x_words, x_scales, w1, tau, sl, 
             nc.scalar.activation(ea[t], sq_win[t][:].indirect(n1_sb[:]), ACT.Exp, scale=neg_tau[:, t : t + 1])
         pieces = [(t, 0, S) for t in range(PACK - 1)] + [(PACK - 1, 0, S // 2), (PACK - 1, S // 2, S)]
         for t, lo, hi in pieces:
-            nc.scalar.activation(y_n2[t][:, lo:hi], y_win[t][:].indirect(n2_sb[:, lo // 16 : hi // 16]), ACT.Copy)
-        warm1 = sbuf("warm1", [P, 1], F32)
-        nc.scalar.activation(warm1[:], y_n2[PACK - 1][:, S - 1 : S], ACT.Sigmoid)
+            nc.scalar.activation(y_n2[t][:, lo:hi], y_win[t][:].indirect(n2_sb[:, lo // GROUP : hi // GROUP]), ACT.Copy)
+        preload_again = sbuf("preload_again", [P, 1], F32)
+        nc.scalar.activation(preload_again[:], y_n2[PACK - 1][:, S - 1 : S], ACT.Sigmoid)
         damped = four("damped", [P, S], F32)
         z_rows = [sbuf("z_rows%d" % a, [P, PACK, S // 2], BF16) for a in range(2)]
         for t in range(PACK):
-            nc.vector.scalar_tensor_tensor(damped[t][:], y_ps[t][:], ga_sb[:, t : t + 1], ea[t], ALU.mult, ALU.mult)
+            nc.vector.scalar_tensor_tensor(damped[t][:], y[t], ga_sb[:, t : t + 1], ea[t], ALU.mult, ALU.mult)
             if t == 0:
                 nc.vector.quantize_mx(out=z2_codes[:].bitcast(FP8X4), scales=z2_scales[:], in_=z2_bf[:])
 
@@ -178,7 +194,7 @@ def tile_picked_selfegaebledb_none_p_kernel(tc, x_words, x_scales, w1, tau, sl, 
         z_bf = four("z_bf", [P, P * PACK], BF16)
         z_codes = four("z_codes", [P, P], U32)
         z_scales = four("z_scales", [P, P], U8)
-        s_ps = [psum.tile([P, S], F32, name="s_ps%d" % u) for u in range(PACK)]
+
         def pack_z(u, lo, hi):
             nc.vector.tensor_copy(
                 out=z_bf[u][:, PACK * lo : PACK * hi].rearrange("p (c i t) -> p c t i", i=4, t=PACK),
@@ -204,10 +220,11 @@ def tile_picked_selfegaebledb_none_p_kernel(tc, x_words, x_scales, w1, tau, sl, 
         pack_z(0, P // 2, P)
         product(0, s_ps[0], 0, S // 2)
         product(0, y_ps[0], S // 2, S)
-        for u in range(1, PACK):
-            if u == 2:
-                for t in range(PACK):
-                    sum_z(1, t, 0, S)
+        pack_z(1, 0, P)
+        product(1, s_ps[1], 0, S)
+        for t in range(PACK):
+            sum_z(1, t, 0, S)
+        for u in (2, 3):
             pack_z(u, 0, P)
             product(u, s_ps[u], 0, S)
 
@@ -221,7 +238,7 @@ def tile_picked_selfegaebledb_none_p_kernel(tc, x_words, x_scales, w1, tau, sl, 
             nc.scalar.activation(sg2_win[u][:, :S], s_win[u][:].indirect(n5_sb[:]), ACT.Sigmoid, bias=bias_sg2[:, col], scale=sl2_sb[:, col])
 
         def finish(u, lo, hi):
-            nc.scalar.activation(sg2_n6[u][:, lo:hi], sg2_win[u][:].indirect(n6_sb[:, lo // 16 : hi // 16]), ACT.Copy)
+            nc.scalar.activation(sg2_n6[u][:, lo:hi], sg2_win[u][:].indirect(n6_sb[:, lo // GROUP : hi // GROUP]), ACT.Copy)
             nc.vector.tensor_tensor(diff[u][:, lo:hi], sg2_win[u][:, lo:hi], sg2_n6[u][:, lo:hi], ALU.subtract)
             nc.vector.scalar_tensor_tensor(res[u][:, lo:hi], diff[u][:, lo:hi], 1.5, s_win[u][:, lo:hi], ALU.mult, ALU.mult)
             nc.sync.dma_start(out=out_rows[u][:, lo:hi], in_=res[u][:, lo:hi])

from contextlib import ExitStack

import concourse.mybir as mybir

K, T, S, H = 512, 2048, 512, 512
FLOPS = 2 * K * H * S + 2 * H * S * S

F32 = mybir.dt.float32
BF16 = mybir.dt.bfloat16
I32 = mybir.dt.int32
U32 = mybir.dt.uint32
U16 = mybir.dt.uint16
U8 = mybir.dt.uint8
FP8X4 = mybir.dt.float8_e4m3fn_x4
ALU = mybir.AluOpType
ACT = mybir.ActivationFunctionType

P = 128
PACK = 4
GROUP = 16
WIDE = 2 * S
W_SPLIT = 56
HALVES = ((0, S // 2), (S // 2, S))


def tile_picked_selfegaebledb_none_p_kernel(tc, x_words, x_scales, w1, tau, sl, th, ga, gb, sl2, th2, offs, n1, n2, n3, n4, n5, n6, out):
    nc = tc.nc
    with ExitStack() as ctx:
        keep = ctx.enter_context(tc.tile_pool(name="keep", bufs=1))
        psum = ctx.enter_context(tc.psum_pool(name="psum", bufs=1))

        def sbuf(name, shape, dtype):
            return keep.tile(shape, dtype, name=name, align_bytes=64)

        def four(name, shape, dtype):
            return [sbuf("%s%d" % (name, t), shape, dtype) for t in range(PACK)]

        def load_list(name, src):
            tile = sbuf(name, [P, S // GROUP], U16)
            nc.sync.dma_start(tile[:], src)
            return tile

        def load_rows(name, src):
            tile = sbuf(name, [P, PACK], F32)
            nc.sync.dma_start(out=tile[:], in_=src.rearrange("(p t) o -> p (t o)", t=PACK))
            return tile

        x_bytes = sbuf("x_bytes", [P, T], U8)
        nc.vector.memset(x_bytes[:].bitcast(I32), 0)
        offs_sb = load_list("offs_sb", offs)
        w_raw = sbuf("w_raw", [P, PACK, H], F32)
        nc.sync.dma_start(out=w_raw[:], in_=w1.rearrange("(p j) c -> p j c", j=PACK))
        sl_sb = load_rows("sl_sb", sl)
        th_sb = load_rows("th_sb", th)
        x_packed = sbuf("x_packed", [P, T], U32)
        nc.sync.dma_start(out=x_packed[:].bitcast(I32), in_=x_words[0].rearrange("p n r -> p (n r)").bitcast(I32))
        for quad in range(4):
            nc.scalar.dma_start(
                out=x_bytes[32 * quad : 32 * quad + 4, :].bitcast(I32),
                in_=x_scales[0, 4 * quad : 4 * quad + 4, :].bitcast(I32),
            )
        n4_sb = load_list("n4_sb", n4)
        gb_sb = load_rows("gb_sb", gb)
        n3_sb = load_list("n3_sb", n3)
        tau_sb = load_rows("tau_sb", tau)
        n1_sb = load_list("n1_sb", n1)
        ga_sb = load_rows("ga_sb", ga)
        n2_sb = load_list("n2_sb", n2)
        sl2_sb = load_rows("sl2_sb", sl2)
        th2_sb = load_rows("th2_sb", th2)
        n5_sb = load_list("n5_sb", n5)
        n6_sb = load_list("n6_sb", n6)

        def times(name, src, factor):
            tile = sbuf(name, [P, PACK], F32)
            nc.gpsimd.tensor_scalar(tile[:], src[:], factor, 0.0, ALU.mult, ALU.add)
            return tile

        def minus_product(name, a, b):
            neg = times(name + "_neg", a, -1.0)
            tile = sbuf(name, [P, PACK], F32)
            nc.gpsimd.tensor_tensor(tile[:], neg[:], b[:], ALU.mult)
            return tile

        bias_sg = minus_product("bias_sg", sl_sb, th_sb)
        neg_tau = times("neg_tau", tau_sb, -1.0)
        half_ga = times("half_ga", ga_sb, -0.5)
        bias_sg2 = minus_product("bias_sg2", sl2_sb, th2_sb)

        y_win = four("y_win", [P, WIDE], F32)
        sq_win = four("sq_win", [P, WIDE], F32)
        s_win = four("s_win", [P, WIDE], F32)
        sg2_win = four("sg2_win", [P, WIDE], F32)
        for t in range(PACK):
            nc.vector.memset(y_win[t][:, S:], 0.0)
        preload_first = sbuf("preload_first", [P, 1], F32)
        nc.scalar.activation(preload_first[:], y_win[0][:, S : S + 1], ACT.Sigmoid)
        sg = [sq_win[PACK - 1 - t][:, S:] for t in range(PACK)]
        y_n2 = [s_win[t][:, S:] for t in range(PACK)]
        ea = [sg2_win[t][:, S:] for t in range(PACK)]

        xq_bytes = sbuf("xq_bytes", [P, S], U8)
        nc.vector.tensor_copy(xq_bytes[:], x_bytes[:].indirect(offs_sb[:]))
        w_bf = sbuf("w_bf", [P, H * PACK], BF16)
        w_dealt = w_bf[:].rearrange("p (a e m j) -> p a m j e", a=2, e=2, j=PACK)
        w_plain = w_raw[:].rearrange("p j (m a e) -> p a m j e", a=2, e=2)
        nc.scalar.copy(
            out=w_bf[:].rearrange("p (t m j) -> p m j t", t=PACK, j=PACK)[:, :W_SPLIT],
            in_=w_raw[:].rearrange("p j (m t) -> p m j t", t=PACK)[:, :W_SPLIT],
        )
        nc.vector.tensor_copy(out=w_dealt[:, :, W_SPLIT:], in_=w_plain[:, :, W_SPLIT:])
        w_codes = sbuf("w_codes", [P, H], U32)
        w_scales = sbuf("w_scales", [P, H], U8)
        nc.vector.quantize_mx(out=w_codes[:].bitcast(FP8X4), scales=w_scales[:], in_=w_bf[:])
        xq_words = sbuf("xq_words", [P, S], U32)
        for lo, hi in HALVES:
            nc.vector.tensor_copy(xq_words[:, lo:hi], x_packed[:].indirect(offs_sb[:, lo // GROUP : hi // GROUP]))

        y_ps = [psum.tile([P, S], F32, name="y_ps%d" % t) for t in range(PACK)]
        s_ps = [psum.tile([P, S], F32, name="s_ps%d" % u) for u in range(PACK)]

        def project(t, bank, lo, hi):
            cols = slice(P * t, P * (t + 1))
            nc.tensor.matmul_mx(
                out=bank[:, lo:hi],
                lhsT=w_codes[:, cols].bitcast(FP8X4),
                lhsT_scale=w_scales[:, cols],
                rhs=xq_words[:, lo:hi].bitcast(FP8X4),
                rhs_scale=xq_bytes[:, lo:hi],
                start=True,
                stop=True,
            )

        for bank, (lo, hi) in zip((s_ps[0], y_ps[0]), HALVES):
            project(0, bank, lo, hi)
            nc.scalar.copy(y_win[0][:, lo:hi], bank[:, lo:hi])
        for t in range(1, PACK):
            project(t, y_ps[t], 0, S)
        y = [y_win[0][:, :S]] + [y_ps[t][:] for t in range(1, PACK)]
        for t in range(1, PACK):
            nc.vector.tensor_copy(y_win[t][:, :S], y_ps[t][:])

        kept = sbuf("kept", [P, PACK, S], F32)
        fetched = sbuf("fetched", [P, PACK, S], F32)
        rest = four("rest", [P, S], F32)
        for t in range(PACK):
            col = slice(t, t + 1)
            nc.scalar.activation(sg[t], y_win[t][:].indirect(n4_sb[:]), ACT.Sigmoid, bias=bias_sg[:, col], scale=sl_sb[:, col])
        nc.gpsimd.tensor_tensor(sq_win[0][:, :S], y_win[0][:, :S], y_win[0][:, :S], ALU.mult)
        for t in range(1, PACK):
            nc.vector.tensor_tensor(sq_win[t][:, :S], y_ps[t][:], y_win[t][:, :S], ALU.mult)
        for t in range(PACK):
            col = slice(t, t + 1)
            nc.vector.tensor_scalar(rest[t][:], sg[t], 1.0, gb_sb[:, col], ALU.subtract, ALU.mult)
            nc.vector.scalar_tensor_tensor(kept[:, t, :], y[t], gb_sb[:, col], sg[t], ALU.mult, ALU.mult)
            nc.vector.tensor_tensor(fetched[:, t, :], y_win[t][:].indirect(n3_sb[:]), rest[t][:], ALU.mult)
        z2_bf = sbuf("z2_bf", [P, S * PACK], BF16)
        nc.vector.tensor_tensor(
            z2_bf[:].rearrange("p (c i t) -> p c t i", i=2, t=PACK),
            kept[:].rearrange("p t (c i) -> p c t i", i=2),
            fetched[:].rearrange("p t (c i) -> p c t i", i=2),
            ALU.subtract,
        )
        z2_codes = sbuf("z2_codes", [P, S], U32)
        z2_scales = sbuf("z2_scales", [P, S], U8)

        for t in range(PACK):
            nc.scalar.activation(ea[t], sq_win[t][:].indirect(n1_sb[:]), ACT.Exp, scale=neg_tau[:, t : t + 1])
        pieces = [(t, 0, S) for t in range(PACK - 1)] + [(PACK - 1, 0, S // 2), (PACK - 1, S // 2, S)]
        for t, lo, hi in pieces:
            nc.scalar.activation(y_n2[t][:, lo:hi], y_win[t][:].indirect(n2_sb[:, lo // GROUP : hi // GROUP]), ACT.Copy)
        preload_again = sbuf("preload_again", [P, 1], F32)
        nc.scalar.activation(preload_again[:], y_n2[PACK - 1][:, S - 1 : S], ACT.Sigmoid)
        damped = four("damped", [P, S], F32)
        z_rows = [sbuf("z_rows%d" % a, [P, PACK, S // 2], BF16) for a in range(2)]
        for t in range(PACK):
            nc.vector.scalar_tensor_tensor(damped[t][:], y[t], ga_sb[:, t : t + 1], ea[t], ALU.mult, ALU.mult)
            if t == 0:
                nc.vector.quantize_mx(out=z2_codes[:].bitcast(FP8X4), scales=z2_scales[:], in_=z2_bf[:])

        def sum_z(a, t, lo, hi):
            nc.vector.scalar_tensor_tensor(
                z_rows[a][:, t, :].rearrange("p (e m) -> p m e", e=2)[:, lo // PACK : hi // PACK],
                y_n2[t][:, lo:hi].rearrange("p (m u) -> p m u", u=PACK)[:, :, 2 * a : 2 * a + 2],
                half_ga[:, t : t + 1],
                damped[t][:, lo:hi].rearrange("p (m u) -> p m u", u=PACK)[:, :, 2 * a : 2 * a + 2],
                ALU.mult,
                ALU.add,
            )

        for t, lo, hi in pieces:
            sum_z(0, t, lo, hi)

        z_bf = four("z_bf", [P, P * PACK], BF16)
        z_codes = four("z_codes", [P, P], U32)
        z_scales = four("z_scales", [P, P], U8)

        def pack_z(u, lo, hi):
            nc.vector.tensor_copy(
                out=z_bf[u][:, PACK * lo : PACK * hi].rearrange("p (c i t) -> p c t i", i=4, t=PACK),
                in_=z_rows[u // 2][:, :, P * (u % 2) + lo : P * (u % 2) + hi].rearrange("p t (c i) -> p c t i", i=4),
            )
            nc.vector.quantize_mx(
                out=z_codes[u][:, lo:hi].bitcast(FP8X4), scales=z_scales[u][:, lo:hi], in_=z_bf[u][:, PACK * lo : PACK * hi]
            )

        def product(u, bank, lo, hi):
            nc.tensor.matmul_mx(
                out=bank[:, lo:hi],
                lhsT=z_codes[u][:].bitcast(FP8X4),
                lhsT_scale=z_scales[u][:],
                rhs=z2_codes[:, lo:hi].bitcast(FP8X4),
                rhs_scale=z2_scales[:, lo:hi],
                start=True,
                stop=True,
            )
            nc.vector.tensor_scalar(s_win[u][:, lo:hi], bank[:, lo:hi], 0.0625, None, ALU.mult)

        pack_z(0, 0, P // 2)
        pack_z(0, P // 2, P)
        product(0, s_ps[0], 0, S // 2)
        product(0, y_ps[0], S // 2, S)
        pack_z(1, 0, P)
        product(1, s_ps[1], 0, S)
        for t in range(PACK):
            sum_z(1, t, 0, S)
        for u in (2, 3):
            pack_z(u, 0, P)
            product(u, s_ps[u], 0, S)

        sg2_n6 = four("sg2_n6", [P, S], F32)
        diff = [sbuf("z_rows1", [P, S], F32)] + [sbuf("diff%d" % u, [P, S], F32) for u in range(1, PACK)]
        res = four("res", [P, S], F32)
        out_rows = out.rearrange("(p u) c -> u p c", u=PACK)

        def gate(u):
            col = slice(u, u + 1)
            nc.scalar.activation(sg2_win[u][:, :S], s_win[u][:].indirect(n5_sb[:]), ACT.Sigmoid, bias=bias_sg2[:, col], scale=sl2_sb[:, col])

        def finish(u, lo, hi):
            nc.scalar.activation(sg2_n6[u][:, lo:hi], sg2_win[u][:].indirect(n6_sb[:, lo // GROUP : hi // GROUP]), ACT.Copy)
            nc.vector.tensor_tensor(diff[u][:, lo:hi], sg2_win[u][:, lo:hi], sg2_n6[u][:, lo:hi], ALU.subtract)
            nc.vector.scalar_tensor_tensor(res[u][:, lo:hi], diff[u][:, lo:hi], 1.5, s_win[u][:, lo:hi], ALU.mult, ALU.mult)
            nc.sync.dma_start(out=out_rows[u][:, lo:hi], in_=res[u][:, lo:hi])

        gate(0)
        gate(1)
        finish(0, 0, S)
        gate(2)
        finish(1, 0, S)
        finish(2, 0, S // 2)
        gate(3)
        finish(2, S // 2, S)
        finish(3, 0, S // 2)
        finish(3, S // 2, S)
